import numpy as np
import ml_dtypes


def mxq(x, axis, fmt="e4m3"):
    dtype, down = {"e4m3": (ml_dtypes.float8_e4m3fn, 7), "e5m2": (ml_dtypes.float8_e5m2, 14)}[fmt]
    v = np.moveaxis(np.asarray(x, np.float32).astype(ml_dtypes.bfloat16).astype(np.float64), axis, -1)
    blocks = v.reshape(v.shape[:-1] + (-1, 32))
    amax = np.abs(blocks).max(-1, keepdims=True)
    byte = np.maximum(np.where(amax > 0, np.frexp(amax)[1] - 1 + 127, 0) - down, 1)
    scale = np.exp2(byte - 127.0)
    codes = (blocks / scale).astype(np.float32).astype(dtype).astype(np.float64)
    return np.moveaxis((codes * scale).reshape(v.shape), -1, axis)


WIDE = False


def mx_kscale(k):
    if not WIDE:
        return np.ones(k)
    levels = np.array([10, -10, 5, -5, 0])
    if k % 512:
        return np.exp2(np.random.permutation(np.resize(levels, k // 32))).repeat(32)
    a = np.empty((k // 512, 16))
    for p in range(k // 512):
        a[p, :8] = np.random.permutation(np.resize(levels, 8))
        for g in range(8):
            far = levels[np.abs(levels - a[p, g]) >= 10]
            a[p, g + 8] = far[np.random.randint(len(far))]
    return np.exp2(a.ravel()).repeat(32)


def f64(x):
    return np.asarray(x).astype(np.float64)


def striped(idx):
    return np.tile(idx.reshape(-1, 16).T, (8, 1)).astype(np.uint16)


def unstriped(offs):
    return offs[:16].T.reshape(-1).astype(np.int64)


def silu(v):
    return v / (1.0 + np.exp(-np.maximum(v, -700.0)))


K, T, D, S, V, H, N = 512, 2048, 4, 1024, 512, 512, 512


def setup_inputs():
    n = np.random.standard_normal
    s = mx_kscale(K)[:, None]
    u = mx_kscale(H)
    return {
        "xT": (n((K, T)) * s).astype(np.float32),
        "w1": (n((K, H)) / np.sqrt(K) / s * u).astype(np.float32),
        "w2": (n((H, N)) / np.sqrt(H) / u[:, None]).astype(np.float32),
        "gate": np.tile(np.random.uniform(0.2, 1.0, (D, 1, V)) / np.sqrt(D), (1, N, 1)).astype(np.float32),
        "offs": striped(np.random.permutation(T)[:S]),
        "pos1": striped(np.random.permutation(S)[:V]),
        "pos2": striped(np.random.permutation(S)[:V]),
        "pos3": striped(np.random.permutation(S)[:V]),
        "pos4": striped(np.random.permutation(S)[:V]),
    }


def reference(xT, w1, w2, gate, offs, pos1, pos2, pos3, pos4):
    idx = unstriped(offs)
    xq = mxq(f64(xT)[:, idx], 0, "e4m3")
    h = silu(mxq(f64(w1), 0, "e4m3").T @ xq)
    y = mxq(f64(w2), 0, "e4m3").T @ mxq(h, 0, "e4m3")
    return sum(f64(gate[d]) * y[:, unstriped(p)] for d, p in enumerate((pos1, pos2, pos3, pos4)))

@@ -1,0 +1,222 @@
+from contextlib import ExitStack
+
+import concourse.mybir as mybir
+
+K, T, D, S, V, H, N = 512, 2048, 4, 1024, 512, 512, 512
+
+FLOPS = 2 * S * (K * H + H * N)
+BYTES = 4 * (K * S + K * H + H * N + D * V + N * V) + 2 * 128 * (S + D * V) // 16
+
+F32 = mybir.dt.float32
+BF16 = mybir.dt.bfloat16
+U32 = mybir.dt.uint32
+U16 = mybir.dt.uint16
+U8 = mybir.dt.uint8
+FP8X4 = mybir.dt.float8_e4m3fn_x4
+MULT = mybir.AluOpType.mult
+ADD = mybir.AluOpType.add
+COPY = mybir.ActivationFunctionType.Copy
+SILU = mybir.ActivationFunctionType.Silu
+
+P = 128
+SLICE = 256
+GROUP = 128
+CHUNK = 512
+
+
+def tile_picked_sub_mlp_silu_sub_e_kernel(
+    tc, xT, w1, w2, gate, offs, pos1, pos2, pos3, pos4, out
+):
+    nc = tc.nc
+    with ExitStack() as ctx:
+        keep = ctx.enter_context(tc.tile_pool(name="keep", bufs=1))
+        prods = ctx.enter_context(tc.tile_pool(name="prods", bufs=8))
+        stage = ctx.enter_context(tc.tile_pool(name="stage", bufs=3))
+        psum_a = ctx.enter_context(tc.psum_pool(name="psum_a", bufs=2))
+        psum_y = ctx.enter_context(tc.psum_pool(name="psum_y", bufs=6))
+
+        warm = keep.tile([P, 1], F32, name="warm")
+        nc.vector.memset(warm[:], 0.0)
+        nc.scalar.activation(warm[:], warm[:], SILU)
+
+        x_rows = xT.rearrange("(p u e) t -> p u e t", u=2, e=2)
+        x_raw = {}
+
+        def load_x(u, c):
+            x_raw[u, c] = keep.tile([P, 2, CHUNK], F32, name=f"x_raw_{u}_{c}")
+            nc.sync.dma_start(x_raw[u, c][:], x_rows[:, u, :, c * CHUNK : (c + 1) * CHUNK])
+
+        load_x(0, 0)
+        offs_sb = keep.tile([P, S // 16], U16, name="offs_sb")
+        nc.sync.dma_start(offs_sb[:], offs)
+        for c in range(1, 4):
+            load_x(0, c)
+        w1_raw = keep.tile([P, 4, H], F32, name="w1_raw")
+        nc.sync.dma_start(w1_raw[:], w1.rearrange("(p j) c -> p j c", j=4))
+        for c in range(4):
+            load_x(1, c)
+        w2_raw = keep.tile([P, 4, N], F32, name="w2_raw")
+        nc.sync.dma_start(w2_raw[:], w2.rearrange("(p j) c -> p j c", j=4))
+        pos_sb = []
+        for d, pos in enumerate((pos1, pos2, pos3, pos4)):
+            pos_tile = keep.tile([P, V // 16], U16, name=f"pos_{d}")
+            nc.sync.dma_start(pos_tile[:], pos)
+            pos_sb.append(pos_tile)
+        gate_sb = keep.tile([P, D, V], F32, name="gate_sb")
+        nc.sync.dma_start(gate_sb[:], gate[:, 0:P, :].rearrange("d p v -> p d v"))
+
+        x_pairs = [keep.tile([P, T, 2], BF16, name=f"x_pairs_{u}", align_bytes=64) for u in range(2)]
+
+        def cast_x(engine, u, c, a, b):
+            dst = x_pairs[u][:, c * CHUNK + a : c * CHUNK + b, :]
+            src = x_raw[u, c][:, :, a:b].rearrange("p e t -> p t e")
+            if engine == "s":
+                nc.scalar.activation(dst, src, COPY)
+            else:
+                nc.vector.tensor_copy(dst, src)
+
+        w1_bf = keep.tile([P, 4 * H], BF16, name="w1_bf", align_bytes=64)
+        w1_codes = keep.tile([P, H], U32, name="w1_codes", align_bytes=64)
+        w1_scales = keep.tile([P, H], U8, name="w1_scales", align_bytes=64)
+        w1_dst = w1_bf[:].rearrange("p (t m j) -> p t m j", t=4, j=4)
+        w1_src = w1_raw[:].rearrange("p j (m t) -> p t m j", t=4)
+
+        xg = keep.tile([P, S * 4], BF16, name="xg", align_bytes=64)
+        xg_words = xg[:].bitcast(U32).rearrange("p (n u) -> p n u", u=2)
+        x_codes = keep.tile([P, S], U32, name="x_codes", align_bytes=64)
+        x_scales = keep.tile([P, S], U8, name="x_scales", align_bytes=64)
+
+        def words(u):
+            return x_pairs[u][:].rearrange("p t e -> p (t e)").bitcast(U32)
+
+        def gather_x(u, n0, n1):
+            nc.vector.tensor_copy(
+                xg_words[:, n0:n1, u], words(u).indirect(offs_sb[:, n0 // 16 : n1 // 16])
+            )
+
+        def quantize(codes, scales, src, n0, n1):
+            nc.vector.quantize_mx(
+                out=codes[:, n0:n1].bitcast(FP8X4), scales=scales[:, n0:n1], in_=src[:, 4 * n0 : 4 * n1]
+            )
+
+        cast_x("s", 0, 0, 0, CHUNK)
+        cast_x("v", 0, 1, 0, CHUNK)
+        cast_x("s", 0, 2, 0, CHUNK)
+        cast_x("v", 0, 3, 0, CHUNK)
+        gather_x(0, 0, S)
+        nc.scalar.activation(w1_dst[:, 0:2], w1_src[:, 0:2], COPY)
+        nc.vector.tensor_copy(w1_dst[:, 2:4], w1_src[:, 2:4])
+        quantize(w1_codes, w1_scales, w1_bf, 0, H)
+        cast_x("s", 1, 0, 0, CHUNK)
+        cast_x("v", 1, 1, 0, CHUNK)
+        cast_x("s", 1, 2, 0, CHUNK)
+        cast_x("s", 1, 3, 0, 160)
+        cast_x("v", 1, 3, 160, CHUNK)
+
+        slices = [(s * SLICE, (s + 1) * SLICE) for s in range(S // SLICE)]
+        gather_x(1, *slices[0])
+        for s in range(len(slices)):
+            if s + 1 < len(slices):
+                gather_x(1, *slices[s + 1])
+            quantize(x_codes, x_scales, xg, *slices[s])
+
+        w2_bf = keep.tile([P, 4 * N], BF16, name="w2_bf", align_bytes=64)
+        w2_codes = keep.tile([P, N], U32, name="w2_codes", align_bytes=64)
+        w2_scales = keep.tile([P, N], U8, name="w2_scales", align_bytes=64)
+        nc.vector.tensor_copy(
+            w2_bf[:].rearrange("p (c j) -> p c j", j=4), w2_raw[:].rearrange("p j c -> p c j")
+        )
+        h_bf = keep.tile([P, S * 4], BF16, name="h_bf", align_bytes=64)
+        h_codes = keep.tile([P, S], U32, name="h_codes", align_bytes=64)
+        h_scales = keep.tile([P, S], U8, name="h_scales", align_bytes=64)
+        y = [keep.tile([P, S], F32, name=f"y_{m}", align_bytes=64) for m in range(4)]
+        y_ps = {}
+
+        def mm(dst, w_codes, w_scales, m, codes, scales, n0, n1):
+            nc.tensor.matmul_mx(
+                out=dst,
+                lhsT=w_codes[:, m * P : (m + 1) * P].bitcast(FP8X4),
+                lhsT_scale=w_scales[:, m * P : (m + 1) * P],
+                rhs=codes[:, n0:n1].bitcast(FP8X4),
+                rhs_scale=scales[:, n0:n1],
+                start=True,
+                stop=True,
+            )
+
+        def layer1(g):
+            n0, n1 = g * GROUP, (g + 1) * GROUP
+            h_ps = psum_a.tile([P, 4, GROUP], F32, name="bank_a")
+            for t in range(4):
+                mm(h_ps[:, t, :], w1_codes, w1_scales, t, x_codes, x_scales, n0, n1)
+            nc.scalar.activation(
+                h_bf[:, 4 * n0 : 4 * n1].rearrange("p (n t) -> p n t", t=4),
+                h_ps[:].rearrange("p t n -> p n t"),
+                SILU,
+            )
+
+        def layer2(m, s):
+            n0, n1 = slices[s]
+            half = s // 2
+            if s % 2 == 0:
+                y_ps[m, half] = psum_y.tile([P, 2 * SLICE], F32, name="bank_y")
+            c0 = (s % 2) * SLICE
+            mm(y_ps[m, half][:, c0 : c0 + SLICE], w2_codes, w2_scales, m, h_codes, h_scales, n0, n1)
+
+        def copy_y(engine, m, s0, s1):
+            half = s0 // 2
+            c0 = (s0 % 2) * SLICE
+            width = (s1 - s0) * SLICE
+            dst = y[m][:, s0 * SLICE : s1 * SLICE]
+            src = y_ps[m, half][:, c0 : c0 + width]
+            if engine == "s":
+                nc.scalar.activation(dst, src, COPY)
+            else:
+                nc.vector.tensor_copy(dst, src)
+
+        for s in range(4):
+            layer1(2 * s)
+            layer1(2 * s + 1)
+            if s == 0:
+                quantize(w2_codes, w2_scales, w2_bf, 0, N)
+            quantize(h_codes, h_scales, h_bf, *slices[s])
+            if s < 3:
+                for m in range(4 if s < 2 else 2):
+                    layer2(m, s)
+            if s == 1:
+                copy_y("v", 0, 0, 2)
+        layer2(0, 3)
+        copy_y("v", 0, 2, 3)
+        copy_y("s", 0, 3, 4)
+        layer2(1, 3)
+        copy_y("s", 1, 0, 2)
+        copy_y("s", 1, 2, 4)
+        for m in (2, 3):
+            layer2(m, 2)
+            layer2(m, 3)
+
+        prod = {}
+
+        def gather_y(m, d):
+            prod[m, d] = prods.tile([P, V], F32, name="prod")
+            nc.vector.tensor_tensor(prod[m, d][:], y[m][:].indirect(pos_sb[d][:]), gate_sb[:, d, :], MULT)
+
+        def add(m, a, b, name):
+            r = stage.tile([P, V], F32, name=name)
+            nc.vector.tensor_tensor(r[:], a[:], b[:], ADD)
+            return r
+
+        for m in range(4):
+            gather_y(m, 0)
+            if m > 0:
+                last = add(m - 1, s012, prod[m - 1, 3], "res")
+                nc.sync.dma_start(out[(m - 1) * P : m * P, :], last[:])
+            gather_y(m, 1)
+            gather_y(m, 2)
+            s01 = add(m, prod[m, 0], prod[m, 1], "s01")
+            gather_y(m, 3)
+            s012 = add(m, s01, prod[m, 2], "s012")
+            if m < 2:
+                copy_y("s", m + 2, 0, 2)
+                copy_y("s", m + 2, 2, 4)
+        last = add(3, s012, prod[3, 3], "res")
+        nc.sync.dma_start(out[3 * P : 4 * P, :], last[:])

@@ -1,6 +1,7 @@
 from contextlib import ExitStack
 
 import concourse.mybir as mybir
+from concourse.masks import make_identity
 
 K, T, D, S, V, H, N = 512, 2048, 4, 1024, 512, 512, 512
 
@@ -21,7 +22,6 @@ SILU = mybir.ActivationFunctionType.Silu
 P = 128
 SLICE = 256
 GROUP = 128
-CHUNK = 512
 
 
 def tile_picked_sub_mlp_silu_sub_e_kernel(
@@ -32,29 +32,31 @@ def tile_picked_sub_mlp_silu_sub_e_kernel(
         keep = ctx.enter_context(tc.tile_pool(name="keep", bufs=1))
         prods = ctx.enter_context(tc.tile_pool(name="prods", bufs=8))
         stage = ctx.enter_context(tc.tile_pool(name="stage", bufs=3))
-        psum_a = ctx.enter_context(tc.psum_pool(name="psum_a", bufs=2))
-        psum_y = ctx.enter_context(tc.psum_pool(name="psum_y", bufs=6))
+        psum_a = ctx.enter_context(tc.psum_pool(name="psum_a", bufs=4))
+        psum_y = ctx.enter_context(tc.psum_pool(name="psum_y", bufs=4))
 
         warm = keep.tile([P, 1], F32, name="warm")
         nc.vector.memset(warm[:], 0.0)
         nc.scalar.activation(warm[:], warm[:], SILU)
+        ident = keep.tile([P, P], F32, name="ident")
+        make_identity(nc, ident[:])
 
         x_rows = xT.rearrange("(p u e) t -> p u e t", u=2, e=2)
         x_raw = {}
 
-        def load_x(u, c):
-            x_raw[u, c] = keep.tile([P, 2, CHUNK], F32, name=f"x_raw_{u}_{c}")
-            nc.sync.dma_start(x_raw[u, c][:], x_rows[:, u, :, c * CHUNK : (c + 1) * CHUNK])
+        def load_x(u, t0, t1):
+            x_raw[u, t0] = keep.tile([P, 2, t1 - t0], F32, name=f"x_raw_{u}_{t0}")
+            nc.sync.dma_start(x_raw[u, t0][:], x_rows[:, u, :, t0:t1])
 
-        load_x(0, 0)
+        load_x(0, 0, 512)
         offs_sb = keep.tile([P, S // 16], U16, name="offs_sb")
         nc.sync.dma_start(offs_sb[:], offs)
-        for c in range(1, 4):
-            load_x(0, c)
+        for t0 in (512, 1024, 1536):
+            load_x(0, t0, t0 + 512)
         w1_raw = keep.tile([P, 4, H], F32, name="w1_raw")
         nc.sync.dma_start(w1_raw[:], w1.rearrange("(p j) c -> p j c", j=4))
-        for c in range(4):
-            load_x(1, c)
+        for t0, t1 in ((0, 512), (512, 1024), (1024, 1536), (1536, 1792), (1792, 2048)):
+            load_x(1, t0, t1)
         w2_raw = keep.tile([P, 4, N], F32, name="w2_raw")
         nc.sync.dma_start(w2_raw[:], w2.rearrange("(p j) c -> p j c", j=4))
         pos_sb = []
@@ -67,9 +69,9 @@ def tile_picked_sub_mlp_silu_sub_e_kernel(
 
         x_pairs = [keep.tile([P, T, 2], BF16, name=f"x_pairs_{u}", align_bytes=64) for u in range(2)]
 
-        def cast_x(engine, u, c, a, b):
-            dst = x_pairs[u][:, c * CHUNK + a : c * CHUNK + b, :]
-            src = x_raw[u, c][:, :, a:b].rearrange("p e t -> p t e")
+        def cast_x(engine, u, t0, a, b):
+            dst = x_pairs[u][:, t0 + a : t0 + b, :]
+            src = x_raw[u, t0][:, :, a:b].rearrange("p e t -> p t e")
             if engine == "s":
                 nc.scalar.activation(dst, src, COPY)
             else:
@@ -99,33 +101,45 @@ def tile_picked_sub_mlp_silu_sub_e_kernel(
                 out=codes[:, n0:n1].bitcast(FP8X4), scales=scales[:, n0:n1], in_=src[:, 4 * n0 : 4 * n1]
             )
 
-        cast_x("s", 0, 0, 0, CHUNK)
-        cast_x("v", 0, 1, 0, CHUNK)
-        cast_x("s", 0, 2, 0, CHUNK)
-        cast_x("v", 0, 3, 0, CHUNK)
+        cast_x("s", 0, 0, 0, 512)
+        cast_x("v", 0, 512, 0, 512)
+        cast_x("s", 0, 1024, 0, 512)
+        cast_x("v", 0, 1536, 0, 512)
         gather_x(0, 0, S)
         nc.scalar.activation(w1_dst[:, 0:2], w1_src[:, 0:2], COPY)
         nc.vector.tensor_copy(w1_dst[:, 2:4], w1_src[:, 2:4])
         quantize(w1_codes, w1_scales, w1_bf, 0, H)
-        cast_x("s", 1, 0, 0, CHUNK)
-        cast_x("v", 1, 1, 0, CHUNK)
-        cast_x("s", 1, 2, 0, CHUNK)
-        cast_x("s", 1, 3, 0, 160)
-        cast_x("v", 1, 3, 160, CHUNK)
+        cast_x("s", 1, 0, 0, 512)
+        cast_x("v", 1, 512, 0, 512)
+        cast_x("s", 1, 1024, 0, 512)
+        cast_x("v", 1, 1536, 0, 256)
+        cast_x("s", 1, 1792, 0, 128)
+        cast_x("v", 1, 1792, 128, 256)
 
         slices = [(s * SLICE, (s + 1) * SLICE) for s in range(S // SLICE)]
         gather_x(1, *slices[0])
-        for s in range(len(slices)):
-            if s + 1 < len(slices):
-                gather_x(1, *slices[s + 1])
-            quantize(x_codes, x_scales, xg, *slices[s])
+        quantize(x_codes, x_scales, xg, *slices[0])
+        gather_x(1, *slices[1])
+        gather_x(1, *slices[2])
+        quantize(x_codes, x_scales, xg, *slices[1])
+        gather_x(1, *slices[3])
+        quantize(x_codes, x_scales, xg, *slices[2])
+        quantize(x_codes, x_scales, xg, *slices[3])
 
         w2_bf = keep.tile([P, 4 * N], BF16, name="w2_bf", align_bytes=64)
         w2_codes = keep.tile([P, N], U32, name="w2_codes", align_bytes=64)
         w2_scales = keep.tile([P, N], U8, name="w2_scales", align_bytes=64)
-        nc.vector.tensor_copy(
-            w2_bf[:].rearrange("p (c j) -> p c j", j=4), w2_raw[:].rearrange("p j c -> p c j")
-        )
+        w2_dst = w2_bf[:].rearrange("p (c j) -> p c j", j=4)
+        w2_src = w2_raw[:].rearrange("p j c -> p c j")
+
+        def cast_w2(i):
+            dst, src = w2_dst[:, i * P : (i + 1) * P], w2_src[:, i * P : (i + 1) * P]
+            if i == 0:
+                nc.vector.tensor_copy(dst, src)
+            else:
+                nc.scalar.activation(dst, src, COPY)
+            quantize(w2_codes, w2_scales, w2_bf, i * P, (i + 1) * P)
+
         h_bf = keep.tile([P, S * 4], BF16, name="h_bf", align_bytes=64)
         h_codes = keep.tile([P, S], U32, name="h_codes", align_bytes=64)
         h_scales = keep.tile([P, S], U8, name="h_scales", align_bytes=64)
@@ -154,45 +168,40 @@ def tile_picked_sub_mlp_silu_sub_e_kernel(
                 SILU,
             )
 
-        def layer2(m, s):
-            n0, n1 = slices[s]
-            half = s // 2
-            if s % 2 == 0:
-                y_ps[m, half] = psum_y.tile([P, 2 * SLICE], F32, name="bank_y")
-            c0 = (s % 2) * SLICE
-            mm(y_ps[m, half][:, c0 : c0 + SLICE], w2_codes, w2_scales, m, h_codes, h_scales, n0, n1)
+        def layer2(m, n0, n1):
+            bank = psum_y.tile([P, 512], F32, name="bank_y")
+            for a in range(n0, n1, SLICE):
+                b = min(a + SLICE, n1)
+                mm(bank[:, a - n0 : b - n0], w2_codes, w2_scales, m, h_codes, h_scales, a, b)
+            return bank
 
-        def copy_y(engine, m, s0, s1):
-            half = s0 // 2
-            c0 = (s0 % 2) * SLICE
-            width = (s1 - s0) * SLICE
-            dst = y[m][:, s0 * SLICE : s1 * SLICE]
-            src = y_ps[m, half][:, c0 : c0 + width]
+        def copy_y(engine, m, bank, n0, n1):
+            dst, src = y[m][:, n0:n1], bank[:, 0 : n1 - n0]
             if engine == "s":
                 nc.scalar.activation(dst, src, COPY)
             else:
                 nc.vector.tensor_copy(dst, src)
 
-        for s in range(4):
-            layer1(2 * s)
-            layer1(2 * s + 1)
-            if s == 0:
-                quantize(w2_codes, w2_scales, w2_bf, 0, N)
-            quantize(h_codes, h_scales, h_bf, *slices[s])
-            if s < 3:
-                for m in range(4 if s < 2 else 2):
-                    layer2(m, s)
-            if s == 1:
-                copy_y("v", 0, 0, 2)
-        layer2(0, 3)
-        copy_y("v", 0, 2, 3)
-        copy_y("s", 0, 3, 4)
-        layer2(1, 3)
-        copy_y("s", 1, 0, 2)
-        copy_y("s", 1, 2, 4)
-        for m in (2, 3):
-            layer2(m, 2)
-            layer2(m, 3)
+        for g in (0, 1):
+            layer1(g)
+        quantize(h_codes, h_scales, h_bf, 0, 256)
+        for g in (2, 3):
+            layer1(g)
+        quantize(h_codes, h_scales, h_bf, 256, 512)
+        cast_w2(0)
+        copy_y("v", 0, layer2(0, 0, 512), 0, 512)
+        for g in (4, 5):
+            layer1(g)
+        quantize(h_codes, h_scales, h_bf, 512, 768)
+        copy_y("v", 0, layer2(0, 512, 768), 512, 768)
+        for n0 in (768, 896):
+            layer1(n0 // GROUP)
+            quantize(h_codes, h_scales, h_bf, n0, n0 + GROUP)
+            copy_y("v", 0, layer2(0, n0, n0 + GROUP), n0, n0 + GROUP)
+        for m in (1, 2, 3):
+            cast_w2(m)
+            for n0 in (0, 512):
+                copy_y("s", m, layer2(m, n0, n0 + 512), n0, n0 + 512)
 
         prod = {}
 
@@ -200,23 +209,42 @@ def tile_picked_sub_mlp_silu_sub_e_kernel(
             prod[m, d] = prods.tile([P, V], F32, name="prod")
             nc.vector.tensor_tensor(prod[m, d][:], y[m][:].indirect(pos_sb[d][:]), gate_sb[:, d, :], MULT)
 
-        def add(m, a, b, name):
-            r = stage.tile([P, V], F32, name=name)
-            nc.vector.tensor_tensor(r[:], a[:], b[:], ADD)
-            return r
+        def pe_sum(m, count):
+            acc_ps = psum_a.tile([P, 4, P], F32, name="bank_a")
+            for b in range(4):
+                for d in range(count):
+                    nc.tensor.matmul(
+                        acc_ps[:, b, :],
+                        prod[m, d][:, b * P : (b + 1) * P],
+                        ident[:],
+                        start=(d == 0),
+                        stop=(d == count - 1),
+                        is_transpose=True,
+                    )
+            acc = stage.tile([P, 4, P], F32, name="acc")
+            nc.scalar.activation(acc[:], acc_ps[:], COPY)
+            back_ps = psum_a.tile([P, V], F32, name="bank_a")
+            for b in range(4):
+                nc.tensor.transpose(back_ps[:, b * P : (b + 1) * P], acc[:, b, :], ident[:])
+            return back_ps
 
-        for m in range(4):
-            gather_y(m, 0)
-            if m > 0:
-                last = add(m - 1, s012, prod[m - 1, 3], "res")
-                nc.sync.dma_start(out[(m - 1) * P : m * P, :], last[:])
-            gather_y(m, 1)
-            gather_y(m, 2)
-            s01 = add(m, prod[m, 0], prod[m, 1], "s01")
-            gather_y(m, 3)
-            s012 = add(m, s01, prod[m, 2], "s012")
-            if m < 2:
-                copy_y("s", m + 2, 0, 2)
-                copy_y("s", m + 2, 2, 4)
-        last = add(3, s012, prod[3, 3], "res")
-        nc.sync.dma_start(out[3 * P : 4 * P, :], last[:])
+        for m in (0, 1):
+            for d in range(D):
+                gather_y(m, d)
+            total = pe_sum(m, D)
+            res = stage.tile([P, V], F32, name="res")
+            nc.scalar.activation(res[:], total[:], COPY)
+            nc.sync.dma_start(out[m * P : (m + 1) * P, :], res[:])
+        part = {}
+        for m in (2, 3):
+            for d in range(D - 1):
+                gather_y(m, d)
+            part[m] = pe_sum(m, D - 1)
+        for m in (2, 3):
+            gather_y(m, D - 1)
+        for m, width in ((2, V), (3, V // 2)):
+            for v0 in range(0, V, width):
+                cols = slice(v0, v0 + width)
+                res_part = stage.tile([P, width], F32, name="res_part")
+                nc.vector.tensor_tensor(res_part[:], prod[m, D - 1][:, cols], part[m][:, cols], ADD)
+                nc.sync.dma_start(out[m * P : (m + 1) * P, cols], res_part[:])

from contextlib import ExitStack

import concourse.mybir as mybir
from concourse.masks import make_identity

K, T, D, S, V, H, N = 512, 2048, 4, 1024, 512, 512, 512

FLOPS = 2 * S * (K * H + H * N)
BYTES = 4 * (K * S + K * H + H * N + D * V + N * V) + 2 * 128 * (S + D * V) // 16

F32 = mybir.dt.float32
BF16 = mybir.dt.bfloat16
U32 = mybir.dt.uint32
U16 = mybir.dt.uint16
U8 = mybir.dt.uint8
FP8X4 = mybir.dt.float8_e4m3fn_x4
MULT = mybir.AluOpType.mult
ADD = mybir.AluOpType.add
COPY = mybir.ActivationFunctionType.Copy
SILU = mybir.ActivationFunctionType.Silu

P = 128
SLICE = 256
GROUP = 128


def tile_picked_sub_mlp_silu_sub_e_kernel(
    tc, xT, w1, w2, gate, offs, pos1, pos2, pos3, pos4, out
):
    nc = tc.nc
    with ExitStack() as ctx:
        keep = ctx.enter_context(tc.tile_pool(name="keep", bufs=1))
        prods = ctx.enter_context(tc.tile_pool(name="prods", bufs=8))
        stage = ctx.enter_context(tc.tile_pool(name="stage", bufs=3))
        psum_a = ctx.enter_context(tc.psum_pool(name="psum_a", bufs=4))
        psum_y = ctx.enter_context(tc.psum_pool(name="psum_y", bufs=4))

        warm = keep.tile([P, 1], F32, name="warm")
        nc.vector.memset(warm[:], 0.0)
        nc.scalar.activation(warm[:], warm[:], SILU)
        ident = keep.tile([P, P], F32, name="ident")
        make_identity(nc, ident[:])

        x_rows = xT.rearrange("(p u e) t -> p u e t", u=2, e=2)
        x_raw = {}

        def load_x(u, t0, t1):
            x_raw[u, t0] = keep.tile([P, 2, t1 - t0], F32, name=f"x_raw_{u}_{t0}")
            nc.sync.dma_start(x_raw[u, t0][:], x_rows[:, u, :, t0:t1])

        load_x(0, 0, 512)
        offs_sb = keep.tile([P, S // 16], U16, name="offs_sb")
        nc.sync.dma_start(offs_sb[:], offs)
        for t0 in (512, 1024, 1536):
            load_x(0, t0, t0 + 512)
        w1_raw = keep.tile([P, 4, H], F32, name="w1_raw")
        nc.sync.dma_start(w1_raw[:], w1.rearrange("(p j) c -> p j c", j=4))
        for t0, t1 in ((0, 512), (512, 1024), (1024, 1536), (1536, 1792), (1792, 2048)):
            load_x(1, t0, t1)
        w2_raw = keep.tile([P, 4, N], F32, name="w2_raw")
        nc.sync.dma_start(w2_raw[:], w2.rearrange("(p j) c -> p j c", j=4))
        pos_sb = []
        for d, pos in enumerate((pos1, pos2, pos3, pos4)):
            pos_tile = keep.tile([P, V // 16], U16, name=f"pos_{d}")
            nc.sync.dma_start(pos_tile[:], pos)
            pos_sb.append(pos_tile)
        gate_sb = keep.tile([P, D, V], F32, name="gate_sb")
        nc.sync.dma_start(gate_sb[:], gate[:, 0:P, :].rearrange("d p v -> p d v"))

        x_pairs = [keep.tile([P, T, 2], BF16, name=f"x_pairs_{u}", align_bytes=64) for u in range(2)]

        def cast_x(engine, u, t0, a, b):
            dst = x_pairs[u][:, t0 + a : t0 + b, :]
            src = x_raw[u, t0][:, :, a:b].rearrange("p e t -> p t e")
            if engine == "s":
                nc.scalar.activation(dst, src, COPY)
            else:
                nc.vector.tensor_copy(dst, src)

        w1_bf = keep.tile([P, 4 * H], BF16, name="w1_bf", align_bytes=64)
        w1_codes = keep.tile([P, H], U32, name="w1_codes", align_bytes=64)
        w1_scales = keep.tile([P, H], U8, name="w1_scales", align_bytes=64)
        w1_dst = w1_bf[:].rearrange("p (t m j) -> p t m j", t=4, j=4)
        w1_src = w1_raw[:].rearrange("p j (m t) -> p t m j", t=4)

        xg = keep.tile([P, S * 4], BF16, name="xg", align_bytes=64)
        xg_words = xg[:].bitcast(U32).rearrange("p (n u) -> p n u", u=2)
        x_codes = keep.tile([P, S], U32, name="x_codes", align_bytes=64)
        x_scales = keep.tile([P, S], U8, name="x_scales", align_bytes=64)

        def words(u):
            return x_pairs[u][:].rearrange("p t e -> p (t e)").bitcast(U32)

        def gather_x(u, n0, n1):
            nc.vector.tensor_copy(
                xg_words[:, n0:n1, u], words(u).indirect(offs_sb[:, n0 // 16 : n1 // 16])
            )

        def quantize(codes, scales, src, n0, n1):
            nc.vector.quantize_mx(
                out=codes[:, n0:n1].bitcast(FP8X4), scales=scales[:, n0:n1], in_=src[:, 4 * n0 : 4 * n1]
            )

        cast_x("s", 0, 0, 0, 512)
        cast_x("v", 0, 512, 0, 512)
        cast_x("s", 0, 1024, 0, 512)
        cast_x("v", 0, 1536, 0, 512)
        gather_x(0, 0, S)
        nc.scalar.activation(w1_dst[:, 0:2], w1_src[:, 0:2], COPY)
        nc.vector.tensor_copy(w1_dst[:, 2:4], w1_src[:, 2:4])
        quantize(w1_codes, w1_scales, w1_bf, 0, H)
        cast_x("s", 1, 0, 0, 512)
        cast_x("v", 1, 512, 0, 512)
        cast_x("s", 1, 1024, 0, 512)
        cast_x("v", 1, 1536, 0, 256)
        cast_x("s", 1, 1792, 0, 128)
        cast_x("v", 1, 1792, 128, 256)

        slices = [(s * SLICE, (s + 1) * SLICE) for s in range(S // SLICE)]
        gather_x(1, *slices[0])
        quantize(x_codes, x_scales, xg, *slices[0])
        gather_x(1, *slices[1])
        gather_x(1, *slices[2])
        quantize(x_codes, x_scales, xg, *slices[1])
        gather_x(1, *slices[3])
        quantize(x_codes, x_scales, xg, *slices[2])
        quantize(x_codes, x_scales, xg, *slices[3])

        w2_bf = keep.tile([P, 4 * N], BF16, name="w2_bf", align_bytes=64)
        w2_codes = keep.tile([P, N], U32, name="w2_codes", align_bytes=64)
        w2_scales = keep.tile([P, N], U8, name="w2_scales", align_bytes=64)
        w2_dst = w2_bf[:].rearrange("p (c j) -> p c j", j=4)
        w2_src = w2_raw[:].rearrange("p j c -> p c j")

        def cast_w2(i):
            dst, src = w2_dst[:, i * P : (i + 1) * P], w2_src[:, i * P : (i + 1) * P]
            if i == 0:
                nc.vector.tensor_copy(dst, src)
            else:
                nc.scalar.activation(dst, src, COPY)
            quantize(w2_codes, w2_scales, w2_bf, i * P, (i + 1) * P)

        h_bf = keep.tile([P, S * 4], BF16, name="h_bf", align_bytes=64)
        h_codes = keep.tile([P, S], U32, name="h_codes", align_bytes=64)
        h_scales = keep.tile([P, S], U8, name="h_scales", align_bytes=64)
        y = [keep.tile([P, S], F32, name=f"y_{m}", align_bytes=64) for m in range(4)]
        y_ps = {}

        def mm(dst, w_codes, w_scales, m, codes, scales, n0, n1):
            nc.tensor.matmul_mx(
                out=dst,
                lhsT=w_codes[:, m * P : (m + 1) * P].bitcast(FP8X4),
                lhsT_scale=w_scales[:, m * P : (m + 1) * P],
                rhs=codes[:, n0:n1].bitcast(FP8X4),
                rhs_scale=scales[:, n0:n1],
                start=True,
                stop=True,
            )

        def layer1(g):
            n0, n1 = g * GROUP, (g + 1) * GROUP
            h_ps = psum_a.tile([P, 4, GROUP], F32, name="bank_a")
            for t in range(4):
                mm(h_ps[:, t, :], w1_codes, w1_scales, t, x_codes, x_scales, n0, n1)
            nc.scalar.activation(
                h_bf[:, 4 * n0 : 4 * n1].rearrange("p (n t) -> p n t", t=4),
                h_ps[:].rearrange("p t n -> p n t"),
                SILU,
            )

        def layer2(m, n0, n1):
            bank = psum_y.tile([P, 512], F32, name="bank_y")
            for a in range(n0, n1, SLICE):
                b = min(a + SLICE, n1)
                mm(bank[:, a - n0 : b - n0], w2_codes, w2_scales, m, h_codes, h_scales, a, b)
            return bank

        def copy_y(engine, m, bank, n0, n1):
            dst, src = y[m][:, n0:n1], bank[:, 0 : n1 - n0]
            if engine == "s":
                nc.scalar.activation(dst, src, COPY)
            else:
                nc.vector.tensor_copy(dst, src)

        for g in (0, 1):
            layer1(g)
        quantize(h_codes, h_scales, h_bf, 0, 256)
        for g in (2, 3):
            layer1(g)
        quantize(h_codes, h_scales, h_bf, 256, 512)
        cast_w2(0)
        copy_y("v", 0, layer2(0, 0, 512), 0, 512)
        for g in (4, 5):
            layer1(g)
        quantize(h_codes, h_scales, h_bf, 512, 768)
        copy_y("v", 0, layer2(0, 512, 768), 512, 768)
        for n0 in (768, 896):
            layer1(n0 // GROUP)
            quantize(h_codes, h_scales, h_bf, n0, n0 + GROUP)
            copy_y("v", 0, layer2(0, n0, n0 + GROUP), n0, n0 + GROUP)
        for m in (1, 2, 3):
            cast_w2(m)
            for n0 in (0, 512):
                copy_y("s", m, layer2(m, n0, n0 + 512), n0, n0 + 512)

        prod = {}

        def gather_y(m, d):
            prod[m, d] = prods.tile([P, V], F32, name="prod")
            nc.vector.tensor_tensor(prod[m, d][:], y[m][:].indirect(pos_sb[d][:]), gate_sb[:, d, :], MULT)

        def pe_sum(m, count):
            acc_ps = psum_a.tile([P, 4, P], F32, name="bank_a")
            for b in range(4):
                for d in range(count):
                    nc.tensor.matmul(
                        acc_ps[:, b, :],
                        prod[m, d][:, b * P : (b + 1) * P],
                        ident[:],
                        start=(d == 0),
                        stop=(d == count - 1),
                        is_transpose=True,
                    )
            acc = stage.tile([P, 4, P], F32, name="acc")
            nc.scalar.activation(acc[:], acc_ps[:], COPY)
            back_ps = psum_a.tile([P, V], F32, name="bank_a")
            for b in range(4):
                nc.tensor.transpose(back_ps[:, b * P : (b + 1) * P], acc[:, b, :], ident[:])
            return back_ps

        for m in (0, 1):
            for d in range(D):
                gather_y(m, d)
            total = pe_sum(m, D)
            res = stage.tile([P, V], F32, name="res")
            nc.scalar.activation(res[:], total[:], COPY)
            nc.sync.dma_start(out[m * P : (m + 1) * P, :], res[:])
        part = {}
        for m in (2, 3):
            for d in range(D - 1):
                gather_y(m, d)
            part[m] = pe_sum(m, D - 1)
        for m in (2, 3):
            gather_y(m, D - 1)
        for m, width in ((2, V), (3, V // 2)):
            for v0 in range(0, V, width):
                cols = slice(v0, v0 + width)
                res_part = stage.tile([P, width], F32, name="res_part")
                nc.vector.tensor_tensor(res_part[:], prod[m, D - 1][:, cols], part[m][:, cols], ADD)
                nc.sync.dma_start(out[m * P : (m + 1) * P, cols], res_part[:])
